import numpy as np
import ml_dtypes


def mxq(x, axis, fmt="e4m3"):
    dtype, down = {"e4m3": (ml_dtypes.float8_e4m3fn, 7), "e5m2": (ml_dtypes.float8_e5m2, 14)}[fmt]
    v = np.moveaxis(np.asarray(x, np.float32).astype(ml_dtypes.bfloat16).astype(np.float64), axis, -1)
    blocks = v.reshape(v.shape[:-1] + (-1, 32))
    amax = np.abs(blocks).max(-1, keepdims=True)
    byte = np.maximum(np.where(amax > 0, np.frexp(amax)[1] - 1 + 127, 0) - down, 1)
    scale = np.exp2(byte - 127.0)
    codes = (blocks / scale).astype(np.float32).astype(dtype).astype(np.float64)
    return np.moveaxis((codes * scale).reshape(v.shape), -1, axis)


WIDE = False


def mx_kscale(k):
    if not WIDE:
        return np.ones(k)
    levels = np.array([10, -10, 5, -5, 0])
    if k % 512:
        return np.exp2(np.random.permutation(np.resize(levels, k // 32))).repeat(32)
    a = np.empty((k // 512, 16))
    for p in range(k // 512):
        a[p, :8] = np.random.permutation(np.resize(levels, 8))
        for g in range(8):
            far = levels[np.abs(levels - a[p, g]) >= 10]
            a[p, g + 8] = far[np.random.randint(len(far))]
    return np.exp2(a.ravel()).repeat(32)


def f64(x):
    return np.asarray(x).astype(np.float64)


def striped(idx):
    return np.tile(idx.reshape(-1, 16).T, (8, 1)).astype(np.uint16)


def unstriped(offs):
    return offs[:16].T.reshape(-1).astype(np.int64)


E2M1 = np.array([0.0, 0.5, 1.0, 1.5, 2.0, 3.0, 4.0, 6.0, -0.0, -0.5, -1.0, -1.5, -2.0, -3.0, -4.0, -6.0])


def pack_weight(w, fmt):
    k, n = w.shape
    w = f64(np.asarray(w, np.float32).astype(ml_dtypes.bfloat16)).reshape(k // 32, 32, n)
    amax = np.abs(w).max(1)
    if fmt == "e4m3":
        byte = np.frexp(amax)[1] - 1 + 127 - 7
    else:
        mant, ex = np.frexp(amax / 6.0)
        byte = np.where(mant > 0.5, ex, ex - 1) + 127
    byte = np.clip(np.where(amax > 0, byte, 1), 1, 254)
    scaled = (w * np.exp2(127.0 - byte)[:, None, :]).reshape(k, n).astype(np.float32)
    by_word = np.ascontiguousarray(scaled.reshape(k // 512, 128, 4, n).transpose(0, 1, 3, 2))
    if fmt == "e4m3":
        words = by_word.astype(ml_dtypes.float8_e4m3fn).view(np.uint8)
    else:
        c = by_word.astype(ml_dtypes.float4_e2m1fn).view(np.uint8) & 0xF
        words = (c[..., 0::2] | (c[..., 1::2] << 4)).reshape(k // 512, 128, 2 * n)
    return np.ascontiguousarray(words), np.ascontiguousarray(byte.astype(np.uint8).reshape(k // 512, 16, n))


def unpack_weight(words, scales, fmt):
    g, _, n = scales.shape
    words = np.ascontiguousarray(words).reshape(g, 128, n, -1)
    if fmt == "e4m3":
        vals = words.view(ml_dtypes.float8_e4m3fn).astype(np.float64)
    else:
        nib = np.empty((g, 128, n, 4), np.uint8)
        nib[..., 0::2] = words & 0xF
        nib[..., 1::2] = words >> 4
        vals = E2M1[nib]
    vals = vals * np.repeat(np.exp2(scales.astype(np.float64) - 127.0), 8, axis=1)[..., None]
    return vals.transpose(0, 1, 3, 2).reshape(g * 512, n)


def gelu(v):
    return 0.5 * v * (1.0 + np.tanh(np.sqrt(2.0 / np.pi) * (v + 0.044715 * v**3)))


def bf(x):
    return np.asarray(x, np.float32).astype(ml_dtypes.bfloat16)

def planes(Y):
    n, m = Y.shape
    b = f64(bf(Y)).reshape(n // 32, 32, m)
    amax = np.abs(b).max(1)
    byte = np.clip(np.where(amax > 0, np.frexp(amax)[1] - 1 + 127 - 7, 1), 1, 254)
    codes = (b * np.exp2(127.0 - byte)[:, None, :]).reshape(n, m).astype(np.float32).astype(ml_dtypes.float8_e4m3fn).view(np.uint8)
    words = codes.reshape(n // 512, 128, 4, m).transpose(0, 1, 3, 2)
    return np.ascontiguousarray(words), np.ascontiguousarray(byte.astype(np.uint8).reshape(n // 512, 16, m))


K, T, S, M = 1536, 2048, 1024, 512

def setup_inputs():
    n = np.random.standard_normal
    s = mx_kscale(K)[:, None]
    u = mx_kscale(S)
    e = np.exp(0.8 * n(K))[:, None]
    idx = np.random.permutation(T)[:S]
    tab_words, tab_scales = pack_weight(0.5 * n((K, T)) / np.sqrt(K) * s, "e4m3")
    x = (n((K, M)) * e).astype(np.float32)
    xb_words, xb_scales = pack_weight(f64(x) / s, "e4m3")
    d = np.exp(0.3 * n(S))
    wdT = n((K, T)) * e / np.sqrt(S)
    wdT[:, idx] /= u
    return {
        "tab_words": tab_words, "tab_scales": tab_scales,
        "offs": striped(idx),
        "xb_words": xb_words, "xb_scales": xb_scales,
        "x": x,
        "b": n((S, M)).astype(np.float32),
        "lo": (-d).astype(np.float32),
        "hi": d.astype(np.float32),
        "g": (np.exp(0.3 * n(S)) * u).astype(np.float32),
        "wdT": wdT.astype(np.float32),
    }

def reference(tab_words, tab_scales, offs, xb_words, xb_scales, x, b, lo, hi, g, wdT):
    v = unpack_weight(tab_words, tab_scales, "e4m3")[:, unstriped(offs)]
    xb = unpack_weight(xb_words, xb_scales, "e4m3")
    r = (v.T @ xb) - f64(b)
    c = np.minimum(np.maximum(r, f64(lo)[:, None]), f64(hi)[:, None])
    h = f64(g)[:, None] * c
    wd = f64(wdT)[:, unstriped(offs)]
    y = f64(x) - (mxq(wd, 1, "e4m3") @ mxq(h, 0, "e4m3"))
    words, scales = planes(y)
    return y, words, scales

@@ -1,0 +1,311 @@
+from contextlib import ExitStack
+
+import concourse.mybir as mybir
+from concourse.masks import make_identity
+
+K, T, S, M = 1536, 2048, 1024, 512
+FLOPS = 2 * K * S * M * 2
+
+F32 = mybir.dt.float32
+BF16 = mybir.dt.bfloat16
+I32 = mybir.dt.int32
+U32 = mybir.dt.uint32
+U16 = mybir.dt.uint16
+U8 = mybir.dt.uint8
+FP8X4 = mybir.dt.float8_e4m3fn_x4
+ALU = mybir.AluOpType
+ACT = mybir.ActivationFunctionType
+
+P = 128
+KIB = 1024
+
+
+def tile_list_robust_ct_sweep_kernel(
+    tc, tab_words, tab_scales, offs, xb_words, xb_scales, x, b, lo, hi, g, wdT, out_0, out_1, out_2
+):
+    nc = tc.nc
+    with ExitStack() as ctx:
+        lists = ctx.enter_context(tc.tile_pool(name="lists", bufs=1))
+        held = ctx.enter_context(tc.tile_pool(name="held", bufs=1))
+        arena = ctx.enter_context(tc.tile_pool(name="arena", bufs=1))
+        ring = ctx.enter_context(tc.tile_pool(name="ring", bufs=3))
+        ring2 = ctx.enter_context(tc.tile_pool(name="ring2", bufs=2))
+        sums = ctx.enter_context(tc.psum_pool(name="sums", bufs=5))
+        turned = ctx.enter_context(tc.psum_pool(name="turned", bufs=3))
+
+        def placed(name, shape, dtype, kib):
+            return arena.tile(shape, dtype, name=name, offset=kib * KIB, align_bytes=64)
+
+        offsets = lists.tile([P, S // 16], U16, name="offsets")
+        nc.sync.dma_start(offsets[:], offs)
+
+        tab_scale_window = held.tile([P, T], U8, name="tab_scale_window", align_bytes=64)
+        nc.vector.memset(tab_scale_window[:].bitcast(I32), 0)
+        xb_planes = held.tile([P, 3, M], U8, name="xb_planes", align_bytes=64)
+        nc.gpsimd.memset(xb_planes[:].bitcast(I32), 0)
+        identity = held.tile([P, P], F32, name="identity")
+        make_identity(nc, identity[:])
+
+        def load_tab_words(a):
+            window = placed("tab_window%d" % a, [P, T], I32, 8 * a)
+            nc.sync.dma_start(window[:], tab_words[a].rearrange("p t i -> p (t i)").bitcast(I32))
+            return window
+
+        def load_tab_scales(q):
+            nc.sync.dma_start(
+                tab_scale_window[32 * q : 32 * q + 12, :].bitcast(I32),
+                tab_scales[:, 4 * q : 4 * q + 4, :].bitcast(I32),
+            )
+
+        def load_xb_scales(q):
+            nc.sync.dma_start(
+                xb_planes[32 * q : 32 * q + 4, :, :].bitcast(I32),
+                xb_scales[:, 4 * q : 4 * q + 4, :].rearrange("a r e -> r a e").bitcast(I32),
+            )
+
+        def load_dealt(name, vec):
+            tile = held.tile([P, 2, 4], F32, name=name)
+            nc.sync.dma_start(tile[:], vec.rearrange("(h p t) -> p h t", h=2, t=4))
+            return tile
+
+        def load_rows(name, src, group, kib):
+            tile = placed(name, [P, 4, M], F32, kib)
+            nc.sync.dma_start(tile[:], src[512 * group : 512 * (group + 1), :].rearrange("(p t) m -> p t m", t=4))
+            return tile
+
+        def wd_rows(group):
+            return wdT[512 * group : 512 * (group + 1), :].rearrange("(p t) c -> p t c", t=4)
+
+        def load_single(group, t, kib):
+            tile = placed("wd_window%d_%d" % (group, t), [P, T], F32, kib)
+            nc.sync.dma_start(tile[:], wd_rows(group)[:, t, :])
+            return tile
+
+        def load_pair(group, t, kib):
+            tile = placed("wd_pair%d_%d" % (group, t), [P, 2, T], F32, kib)
+            nc.sync.dma_start(tile[:], wd_rows(group)[:, t : t + 2, :])
+            return tile
+
+        tab_windows = [load_tab_words(0)]
+        load_tab_scales(0)
+        load_tab_scales(1)
+        tab_windows.append(load_tab_words(1))
+        load_tab_scales(2)
+        load_tab_scales(3)
+        tab_windows.append(load_tab_words(2))
+        load_xb_scales(0)
+        load_xb_scales(1)
+        xb_codes = held.tile([P, 3, M], I32, name="xb_codes", align_bytes=64)
+        nc.sync.dma_start(xb_codes[:], xb_words.rearrange("a p e i -> p a (e i)").bitcast(I32))
+        load_xb_scales(2)
+        load_xb_scales(3)
+        WINDOW_KIB = 72
+
+        def window_kib(unit):
+            return WINDOW_KIB + 8 * unit
+
+        windows = []
+
+        def load_windows(count):
+            for unit in range(len(windows), len(windows) + count):
+                windows.append(load_single(unit // 4, unit % 4, window_kib(unit)))
+
+        load_windows(1)
+        lo_sb = load_dealt("lo_sb", lo)
+        b_sb = [load_rows("b0", b, 0, 24)]
+        hi_sb = load_dealt("hi_sb", hi)
+        g_sb = load_dealt("g_sb", g)
+        load_windows(1)
+        b_sb.append(load_rows("b1", b, 1, 32))
+        load_windows(3)
+        x_sb = [load_rows("x0", x, 0, 40)]
+        load_windows(3)
+        x_sb.append(load_rows("x1", x, 1, 48))
+        load_windows(4)
+        x_sb.append(load_rows("x2", x, 2, 56))
+
+        def dealt_view(tile):
+            return tile[:].rearrange("p (h t q) -> p h q t", h=2, t=4)
+
+        picked_words = [placed("picked_words%d" % a, [P, S], U32, 168 + 4 * a) for a in range(3)]
+        picked_scales = held.tile([P, S], U8, name="picked_scales", align_bytes=64)
+        for a in range(2):
+            nc.vector.tensor_copy(dealt_view(picked_words[a]), tab_windows[a][:].bitcast(U32).indirect(offsets[:]))
+        nc.vector.tensor_copy(dealt_view(picked_scales), tab_scale_window[:].indirect(offsets[:]))
+        for h in range(2):
+            nc.vector.tensor_copy(
+                dealt_view(picked_words[2])[:, h], tab_windows[2][:].bitcast(U32).indirect(offsets[:, 32 * h : 32 * (h + 1)])
+            )
+
+        grouped_wd = {}
+        stationary = {}
+
+        def gather_and_turn(unit):
+            picked = ring.tile([P, S], BF16, name="picked_single")
+            nc.vector.tensor_copy(picked[:], windows[unit][:].indirect(offsets[:]))
+            words = picked[:].bitcast(F32)
+            bank = turned.tile([P, 4, P], F32, name="bank")
+            for h in range(2):
+                for u in range(2):
+                    nc.tensor.transpose(bank[:, 2 * h + u, :], words[:, 256 * h + u : 256 * (h + 1) : 2], identity[:])
+            if unit % 2 == 0:
+                grouped_wd[unit // 2] = ring.tile([P, 2 * S], BF16, name="grouped_wd", align_bytes=64)
+            half = grouped_wd[unit // 2][:, S * (unit % 2) : S * (unit % 2 + 1)]
+            nc.scalar.copy(
+                half.bitcast(F32).rearrange("p (h n u) -> p h n u", h=2, u=2),
+                bank[:].rearrange("p (h u) n -> p h n u", h=2),
+            )
+
+        def quantise_wd(unit, count, kib):
+            first = S * (unit % 2)
+            codes = placed("wd_codes%d" % unit, [P, count * 2 * P], U32, kib)
+            scales = held.tile([P, count * 2 * P], U8, name="wd_scales%d" % unit, align_bytes=64)
+            nc.vector.quantize_mx(
+                out=codes[:].bitcast(FP8X4), scales=scales[:], in_=grouped_wd[unit // 2][:, first : first + count * S]
+            )
+            for i in range(count):
+                stationary[unit + i] = (codes, scales, 2 * P * i)
+
+        def interleave(dst, src):
+            nc.scalar.copy(
+                dst[:].rearrange("p (c i t) -> p c t i", i=4, t=4),
+                src[:].rearrange("p t (c i) -> p c t i", i=4),
+            )
+
+        grouped_h = []
+        rounded_h = []
+        residual = []
+
+        def residuals(h):
+            rows = b_sb[h]
+            rounded = ring2.tile([P, 4, M], BF16, name="h_rounded")
+            for t in range(4):
+                cols = slice(512 * h + P * t, 512 * h + P * (t + 1))
+                acc = sums.tile([P, M], F32, name="acc")
+                for a in range(3):
+                    nc.tensor.matmul_mx(
+                        out=acc[:],
+                        lhsT=picked_words[a][:, cols].bitcast(FP8X4),
+                        lhsT_scale=picked_scales[4 * a : P, cols],
+                        rhs=xb_codes[:, a, :].bitcast(FP8X4),
+                        rhs_scale=xb_planes[:, a, :],
+                        start=(a == 0),
+                        stop=(a == 2),
+                    )
+                if False:
+                    staged = placed("staged_r%d_%d" % (h, t), [P, M], F32, 16 + 2 * t)
+                    nc.scalar.copy(staged[:], acc[:])
+                    nc.gpsimd.tensor_tensor(rows[:, t, :], staged[:], rows[:, t, :], ALU.subtract)
+                else:
+                    nc.vector.tensor_tensor(rows[:, t, :], acc[:], rows[:, t, :], ALU.subtract)
+                nc.gpsimd.tensor_scalar(
+                    rows[:, t, :], rows[:, t, :], hi_sb[:, h, t : t + 1], lo_sb[:, h, t : t + 1], ALU.min, ALU.max
+                )
+                nc.gpsimd.tensor_scalar(
+                    rounded[:, t, :], rows[:, t, :], g_sb[:, h, t : t + 1], 0.0, ALU.mult, ALU.add
+                )
+            rounded_h.append(rounded)
+
+        def group_h(h, unit):
+            grouped = placed("h_grouped%d" % h, [P, 4 * M], BF16, window_kib(unit) + 4)
+            interleave(grouped, rounded_h[h])
+            grouped_h.append(grouped)
+
+        def quantise_h(h, unit):
+            codes = placed("h_codes%d" % h, [P, M], U32, window_kib(unit) + 2)
+            scales = held.tile([P, M], U8, name="h_scales%d" % h, align_bytes=64)
+            nc.vector.quantize_mx(out=codes[:].bitcast(FP8X4), scales=scales[:], in_=grouped_h[h][:])
+            residual.append((codes, scales))
+
+        y_planes_early = held.tile([P, M], U8, name="y_planes_early", align_bytes=64)
+        y_plane_last = held.tile([P, M], U8, name="y_plane_last", align_bytes=64)
+        grouped_y = []
+
+        def update(group):
+            rows = x_sb[group]
+            out_rows = out_0[512 * group : 512 * (group + 1), :].rearrange("(p t) m -> p t m", t=4)
+            for t in range(4):
+                codes, scales, first = stationary[4 * group + t]
+                acc = sums.tile([P, M], F32, name="acc")
+                for h in range(2):
+                    cols = slice(first + P * h, first + P * (h + 1))
+                    nc.tensor.matmul_mx(
+                        out=acc[:],
+                        lhsT=codes[:, cols].bitcast(FP8X4),
+                        lhsT_scale=scales[:, cols],
+                        rhs=residual[h][0][:].bitcast(FP8X4),
+                        rhs_scale=residual[h][1][:],
+                        start=(h == 0),
+                        stop=(h == 1),
+                    )
+                if group < 2:
+                    staged = placed("staged_y%d_%d" % (group, t), [P, M], F32, 8 * group + 2 * t)
+                    nc.scalar.copy(staged[:], acc[:])
+                    nc.gpsimd.tensor_tensor(rows[:, t, :], rows[:, t, :], staged[:], ALU.subtract)
+                else:
+                    nc.vector.tensor_tensor(rows[:, t, :], rows[:, t, :], acc[:], ALU.subtract)
+                if group == 2 and t % 2 == 1:
+                        nc.sync.dma_start(out_rows[:, t - 1 : t + 1, :], rows[:, t - 1 : t + 1, :])
+            if group < 2:
+                nc.sync.dma_start(out_rows, rows[:])
+
+        def group_y(group, kib):
+            rows = x_sb[group]
+            grouped = placed("y_grouped%d" % group, [P, 4 * M], BF16, kib)
+            if group < 2:
+                interleave(grouped, rows)
+            else:
+                dst = grouped[:].rearrange("p (c i t) -> p c t i", i=4, t=4)
+                src = rows[:].rearrange("p t (c i) -> p c t i", i=4)
+                nc.scalar.copy(dst[:, 0:48], src[:, 0:48])
+                nc.vector.tensor_copy(dst[:, 48:128], src[:, 48:128])
+            grouped_y.append(grouped)
+
+        def quantise_y(group, kib):
+            codes = placed("y_codes%d" % group, [P, M], I32, kib)
+            plane = y_plane_last[:] if group == 2 else y_planes_early[4 * group : P, :]
+            nc.vector.quantize_mx(out=codes[:].bitcast(FP8X4), scales=plane, in_=grouped_y[group][:])
+            nc.sync.dma_start(out_1[group].rearrange("p m t -> p (m t)").bitcast(I32), codes[:])
+
+        gather_and_turn(0)
+        residuals(0)
+        gather_and_turn(1)
+        group_h(0, 1)
+        residuals(1)
+        gather_and_turn(2)
+        gather_and_turn(3)
+        quantise_wd(0, 2, window_kib(3))
+        quantise_h(0, 3)
+        gather_and_turn(4)
+        group_h(1, 4)
+        gather_and_turn(5)
+        quantise_wd(2, 2, window_kib(5))
+        quantise_h(1, 5)
+        update(0)
+        gather_and_turn(6)
+        quantise_wd(4, 2, window_kib(6))
+        gather_and_turn(7)
+        gather_and_turn(8)
+        quantise_wd(6, 2, window_kib(8))
+        group_y(0, window_kib(8) + 4)
+        update(1)
+        gather_and_turn(9)
+        quantise_y(0, window_kib(9) + 2)
+        gather_and_turn(10)
+        quantise_wd(8, 2, window_kib(10))
+        group_y(1, window_kib(10) + 4)
+        gather_and_turn(11)
+        quantise_wd(10, 1, window_kib(11))
+        quantise_y(1, window_kib(11) + 2)
+        for q in range(4):
+            nc.sync.dma_start(
+                out_2[0:2, 4 * q : 4 * q + 4, :].bitcast(I32), y_planes_early[32 * q : 32 * q + 8, :].bitcast(I32)
+            )
+        quantise_wd(11, 1, 64)
+        update(2)
+        group_y(2, 68)
+        quantise_y(2, 66)
+        for q in range(4):
+            nc.sync.dma_start(
+                out_2[2, 4 * q : 4 * q + 4, :].bitcast(I32), y_plane_last[32 * q : 32 * q + 4, :].bitcast(I32)
+            )

@@ -18,6 +18,7 @@ ACT = mybir.ActivationFunctionType
 
 P = 128
 KIB = 1024
+GP_PARTS = 1
 
 
 def tile_list_robust_ct_sweep_kernel(
@@ -29,9 +30,19 @@ def tile_list_robust_ct_sweep_kernel(
         held = ctx.enter_context(tc.tile_pool(name="held", bufs=1))
         arena = ctx.enter_context(tc.tile_pool(name="arena", bufs=1))
         ring = ctx.enter_context(tc.tile_pool(name="ring", bufs=3))
-        ring2 = ctx.enter_context(tc.tile_pool(name="ring2", bufs=2))
-        sums = ctx.enter_context(tc.psum_pool(name="sums", bufs=5))
-        turned = ctx.enter_context(tc.psum_pool(name="turned", bufs=3))
+        psum = ctx.enter_context(tc.psum_pool(name="psum", bufs=1))
+        sum_banks = []
+        turn_banks = []
+
+        def sum_bank(shape):
+            n = len(sum_banks)
+            sum_banks.append(n)
+            return psum.tile(shape, F32, name="sum_bank%d" % n, offset=2 * KIB * (n % 5))
+
+        def turn_bank(shape):
+            n = len(turn_banks)
+            turn_banks.append(n)
+            return psum.tile(shape, F32, name="turn_bank%d" % n, offset=2 * KIB * (5 + n % 3))
 
         def placed(name, shape, dtype, kib):
             return arena.tile(shape, dtype, name=name, offset=kib * KIB, align_bytes=64)
@@ -39,10 +50,12 @@ def tile_list_robust_ct_sweep_kernel(
         offsets = lists.tile([P, S // 16], U16, name="offsets")
         nc.sync.dma_start(offsets[:], offs)
 
-        tab_scale_window = held.tile([P, T], U8, name="tab_scale_window", align_bytes=64)
+        tab_scale_window = placed("tab_scale_window", [P, T], U8, 176)
         nc.vector.memset(tab_scale_window[:].bitcast(I32), 0)
         xb_planes = held.tile([P, 3, M], U8, name="xb_planes", align_bytes=64)
-        nc.gpsimd.memset(xb_planes[:].bitcast(I32), 0)
+        ray_rows = held.tile([P, M], F32, name="ray_rows")
+        nc.vector.memset(ray_rows[:], 0.0)
+        nc.vector.memset(xb_planes[:].bitcast(I32), 0)
         identity = held.tile([P, P], F32, name="identity")
         make_identity(nc, identity[:])
 
@@ -52,7 +65,7 @@ def tile_list_robust_ct_sweep_kernel(
             return window
 
         def load_tab_scales(q):
-            nc.sync.dma_start(
+            nc.gpsimd.dma_start(
                 tab_scale_window[32 * q : 32 * q + 12, :].bitcast(I32),
                 tab_scales[:, 4 * q : 4 * q + 4, :].bitcast(I32),
             )
@@ -63,10 +76,8 @@ def tile_list_robust_ct_sweep_kernel(
                 xb_scales[:, 4 * q : 4 * q + 4, :].rearrange("a r e -> r a e").bitcast(I32),
             )
 
-        def load_dealt(name, vec):
-            tile = held.tile([P, 2, 4], F32, name=name)
-            nc.sync.dma_start(tile[:], vec.rearrange("(h p t) -> p h t", h=2, t=4))
-            return tile
+        def load_ray_rows(i, vec):
+            nc.sync.dma_start(ray_rows[2 * i : 2 * i + 2, :], vec.rearrange("(h c) -> h c", h=2))
 
         def load_rows(name, src, group, kib):
             tile = placed(name, [P, 4, M], F32, kib)
@@ -86,12 +97,23 @@ def tile_list_robust_ct_sweep_kernel(
             nc.sync.dma_start(tile[:], wd_rows(group)[:, t : t + 2, :])
             return tile
 
-        tab_windows = [load_tab_words(0)]
-        load_tab_scales(0)
-        load_tab_scales(1)
-        tab_windows.append(load_tab_words(1))
-        load_tab_scales(2)
-        load_tab_scales(3)
+        WINDOW_KIB = 72
+
+        def window_kib(unit):
+            return WINDOW_KIB + 8 * unit
+
+        windows = {}
+
+        def load_windows(first, count):
+            for unit in range(first, first + count):
+                windows[unit] = load_single(unit // 4, unit % 4, window_kib(unit))
+
+        for q in range(4):
+            load_tab_scales(q)
+        tab_windows = [load_tab_words(a) for a in range(2)]
+        load_ray_rows(0, lo)
+        load_ray_rows(1, hi)
+        load_ray_rows(2, g)
         tab_windows.append(load_tab_words(2))
         load_xb_scales(0)
         load_xb_scales(1)
@@ -99,30 +121,21 @@ def tile_list_robust_ct_sweep_kernel(
         nc.sync.dma_start(xb_codes[:], xb_words.rearrange("a p e i -> p a (e i)").bitcast(I32))
         load_xb_scales(2)
         load_xb_scales(3)
-        WINDOW_KIB = 72
-
-        def window_kib(unit):
-            return WINDOW_KIB + 8 * unit
-
-        windows = []
-
-        def load_windows(count):
-            for unit in range(len(windows), len(windows) + count):
-                windows.append(load_single(unit // 4, unit % 4, window_kib(unit)))
-
-        load_windows(1)
-        lo_sb = load_dealt("lo_sb", lo)
+        load_windows(0, 1)
         b_sb = [load_rows("b0", b, 0, 24)]
-        hi_sb = load_dealt("hi_sb", hi)
-        g_sb = load_dealt("g_sb", g)
-        load_windows(1)
+        load_windows(1, 1)
         b_sb.append(load_rows("b1", b, 1, 32))
-        load_windows(3)
+        load_windows(2, 3)
         x_sb = [load_rows("x0", x, 0, 40)]
-        load_windows(3)
+        load_windows(5, 3)
         x_sb.append(load_rows("x1", x, 1, 48))
-        load_windows(4)
-        x_sb.append(load_rows("x2", x, 2, 56))
+        load_windows(8, 3)
+        x_last = placed("x2", [P, 4, M], F32, 56)
+        x_last_rows = x[1024:1536, :].rearrange("(p t) m -> p t m", t=4)
+        nc.sync.dma_start(x_last[:, 0:2, :], x_last_rows[:, 0:2, :])
+        load_windows(11, 1)
+        nc.sync.dma_start(x_last[:, 2:4, :], x_last_rows[:, 2:4, :])
+        x_sb.append(x_last)
 
         def dealt_view(tile):
             return tile[:].rearrange("p (h t q) -> p h q t", h=2, t=4)
@@ -137,6 +150,12 @@ def tile_list_robust_ct_sweep_kernel(
                 dealt_view(picked_words[2])[:, h], tab_windows[2][:].bitcast(U32).indirect(offsets[:, 32 * h : 32 * (h + 1)])
             )
 
+        ray_bank = turn_bank([P, 4, P])
+        for t in range(4):
+            nc.tensor.transpose(ray_bank[:, t, :], ray_rows[:, t : M : 4], identity[:])
+        ray_values = held.tile([P, 4, 6], F32, name="ray_values")
+        nc.scalar.copy(ray_values[:], ray_bank[:, :, 0:6])
+
         grouped_wd = {}
         stationary = {}
 
@@ -144,7 +163,7 @@ def tile_list_robust_ct_sweep_kernel(
             picked = ring.tile([P, S], BF16, name="picked_single")
             nc.vector.tensor_copy(picked[:], windows[unit][:].indirect(offsets[:]))
             words = picked[:].bitcast(F32)
-            bank = turned.tile([P, 4, P], F32, name="bank")
+            bank = turn_bank([P, 4, P])
             for h in range(2):
                 for u in range(2):
                     nc.tensor.transpose(bank[:, 2 * h + u, :], words[:, 256 * h + u : 256 * (h + 1) : 2], identity[:])
@@ -173,15 +192,15 @@ def tile_list_robust_ct_sweep_kernel(
             )
 
         grouped_h = []
-        rounded_h = []
+        rounded_h = [held.tile([P, 4, M], BF16, name="h_rounded%d" % h) for h in range(2)]
         residual = []
 
-        def residuals(h):
+        def residuals(h, ts):
             rows = b_sb[h]
-            rounded = ring2.tile([P, 4, M], BF16, name="h_rounded")
-            for t in range(4):
+            rounded = rounded_h[h]
+            for t in ts:
                 cols = slice(512 * h + P * t, 512 * h + P * (t + 1))
-                acc = sums.tile([P, M], F32, name="acc")
+                acc = sum_bank([P, M])
                 for a in range(3):
                     nc.tensor.matmul_mx(
                         out=acc[:],
@@ -192,19 +211,13 @@ def tile_list_robust_ct_sweep_kernel(
                         start=(a == 0),
                         stop=(a == 2),
                     )
-                if False:
-                    staged = placed("staged_r%d_%d" % (h, t), [P, M], F32, 16 + 2 * t)
-                    nc.scalar.copy(staged[:], acc[:])
-                    nc.gpsimd.tensor_tensor(rows[:, t, :], staged[:], rows[:, t, :], ALU.subtract)
-                else:
-                    nc.vector.tensor_tensor(rows[:, t, :], acc[:], rows[:, t, :], ALU.subtract)
+                nc.vector.tensor_tensor(rows[:, t, :], acc[:], rows[:, t, :], ALU.subtract)
                 nc.gpsimd.tensor_scalar(
-                    rows[:, t, :], rows[:, t, :], hi_sb[:, h, t : t + 1], lo_sb[:, h, t : t + 1], ALU.min, ALU.max
+                    rows[:, t, :], rows[:, t, :], ray_values[:, t, 2 + h : 3 + h], ray_values[:, t, h : h + 1], ALU.min, ALU.max
                 )
                 nc.gpsimd.tensor_scalar(
-                    rounded[:, t, :], rows[:, t, :], g_sb[:, h, t : t + 1], 0.0, ALU.mult, ALU.add
+                    rounded[:, t, :], rows[:, t, :], ray_values[:, t, 4 + h : 5 + h], 0.0, ALU.mult, ALU.add
                 )
-            rounded_h.append(rounded)
 
         def group_h(h, unit):
             grouped = placed("h_grouped%d" % h, [P, 4 * M], BF16, window_kib(unit) + 4)
@@ -221,12 +234,14 @@ def tile_list_robust_ct_sweep_kernel(
         y_plane_last = held.tile([P, M], U8, name="y_plane_last", align_bytes=64)
         grouped_y = []
 
-        def update(group):
-            rows = x_sb[group]
+        y_sb = {0: x_sb[0], 1: x_sb[1]}
+
+        def update(group, ts):
+            rows = y_sb[group]
             out_rows = out_0[512 * group : 512 * (group + 1), :].rearrange("(p t) m -> p t m", t=4)
-            for t in range(4):
+            for t in ts:
                 codes, scales, first = stationary[4 * group + t]
-                acc = sums.tile([P, M], F32, name="acc")
+                acc = sum_bank([P, M])
                 for h in range(2):
                     cols = slice(first + P * h, first + P * (h + 1))
                     nc.tensor.matmul_mx(
@@ -239,18 +254,20 @@ def tile_list_robust_ct_sweep_kernel(
                         stop=(h == 1),
                     )
                 if group < 2:
-                    staged = placed("staged_y%d_%d" % (group, t), [P, M], F32, 8 * group + 2 * t)
+                    staged = placed("staged_y%d_%d" % (group, t), [P, M], F32, 8 + 8 * group + 2 * t)
                     nc.scalar.copy(staged[:], acc[:])
-                    nc.gpsimd.tensor_tensor(rows[:, t, :], rows[:, t, :], staged[:], ALU.subtract)
+                    for half in range(GP_PARTS):
+                        cols = slice(half * M // GP_PARTS, (half + 1) * M // GP_PARTS)
+                        nc.gpsimd.tensor_tensor(rows[:, t, cols], rows[:, t, cols], staged[:, cols], ALU.subtract)
+                    if t == 3:
+                        nc.sync.dma_start(out_rows, rows[:])
                 else:
-                    nc.vector.tensor_tensor(rows[:, t, :], rows[:, t, :], acc[:], ALU.subtract)
-                if group == 2 and t % 2 == 1:
+                    nc.vector.tensor_tensor(rows[:, t, :], x_sb[group][:, t, :], acc[:], ALU.subtract)
+                    if t % 2 == 1:
                         nc.sync.dma_start(out_rows[:, t - 1 : t + 1, :], rows[:, t - 1 : t + 1, :])
-            if group < 2:
-                nc.sync.dma_start(out_rows, rows[:])
 
         def group_y(group, kib):
-            rows = x_sb[group]
+            rows = y_sb[group]
             grouped = placed("y_grouped%d" % group, [P, 4 * M], BF16, kib)
             if group < 2:
                 interleave(grouped, rows)
@@ -268,10 +285,10 @@ def tile_list_robust_ct_sweep_kernel(
             nc.sync.dma_start(out_1[group].rearrange("p m t -> p (m t)").bitcast(I32), codes[:])
 
         gather_and_turn(0)
-        residuals(0)
+        residuals(0, range(4))
         gather_and_turn(1)
         group_h(0, 1)
-        residuals(1)
+        residuals(1, range(4))
         gather_and_turn(2)
         gather_and_turn(3)
         quantise_wd(0, 2, window_kib(3))
@@ -281,28 +298,31 @@ def tile_list_robust_ct_sweep_kernel(
         gather_and_turn(5)
         quantise_wd(2, 2, window_kib(5))
         quantise_h(1, 5)
-        update(0)
+        update(0, range(4))
         gather_and_turn(6)
         quantise_wd(4, 2, window_kib(6))
         gather_and_turn(7)
         gather_and_turn(8)
         quantise_wd(6, 2, window_kib(8))
         group_y(0, window_kib(8) + 4)
-        update(1)
+        update(1, range(4))
         gather_and_turn(9)
-        quantise_y(0, window_kib(9) + 2)
         gather_and_turn(10)
         quantise_wd(8, 2, window_kib(10))
+        quantise_y(0, window_kib(10) + 2)
         group_y(1, window_kib(10) + 4)
         gather_and_turn(11)
         quantise_wd(10, 1, window_kib(11))
+        y_sb[2] = placed("y2", [P, 4, M], F32, window_kib(11) + 4)
+        update(2, range(2))
+        quantise_wd(11, 1, 64)
+        update(2, range(2, 3))
         quantise_y(1, window_kib(11) + 2)
         for q in range(4):
             nc.sync.dma_start(
                 out_2[0:2, 4 * q : 4 * q + 4, :].bitcast(I32), y_planes_early[32 * q : 32 * q + 8, :].bitcast(I32)
             )
-        quantise_wd(11, 1, 64)
-        update(2)
+        update(2, range(3, 4))
         group_y(2, 68)
         quantise_y(2, 66)
         for q in range(4):

@@ -37,12 +37,12 @@ def tile_list_robust_ct_sweep_kernel(
         def sum_bank(shape):
             n = len(sum_banks)
             sum_banks.append(n)
-            return psum.tile(shape, F32, name="sum_bank%d" % n, offset=2 * KIB * (n % 5))
+            return psum.tile(shape, F32, name="sum_bank%d" % n, offset=2 * KIB * (n % 4))
 
         def turn_bank(shape):
             n = len(turn_banks)
             turn_banks.append(n)
-            return psum.tile(shape, F32, name="turn_bank%d" % n, offset=2 * KIB * (5 + n % 3))
+            return psum.tile(shape, F32, name="turn_bank%d" % n, offset=2 * KIB * (4 + n % 4))
 
         def placed(name, shape, dtype, kib):
             return arena.tile(shape, dtype, name=name, offset=kib * KIB, align_bytes=64)
@@ -160,28 +160,36 @@ def tile_list_robust_ct_sweep_kernel(
         stationary = {}
 
         def gather_and_turn(unit):
-            picked = ring.tile([P, S], BF16, name="picked_single")
-            nc.vector.tensor_copy(picked[:], windows[unit][:].indirect(offsets[:]))
-            words = picked[:].bitcast(F32)
-            bank = turn_bank([P, 4, P])
-            for h in range(2):
-                for u in range(2):
-                    nc.tensor.transpose(bank[:, 2 * h + u, :], words[:, 256 * h + u : 256 * (h + 1) : 2], identity[:])
-            if unit % 2 == 0:
+            picked = ring.tile([P, S], F32, name="picked_wd")
+            nc.vector.tensor_copy(dealt_view(picked), windows[unit][:].indirect(offsets[:]))
+            if unit == 10:
+                grouped_wd[unit // 2] = placed("grouped_wd_last", [P, 2 * S], BF16, 0)
+            elif unit % 2 == 0:
                 grouped_wd[unit // 2] = ring.tile([P, 2 * S], BF16, name="grouped_wd", align_bytes=64)
-            half = grouped_wd[unit // 2][:, S * (unit % 2) : S * (unit % 2 + 1)]
-            nc.scalar.copy(
-                half.bitcast(F32).rearrange("p (h n u) -> p h n u", h=2, u=2),
-                bank[:].rearrange("p (h u) n -> p h n u", h=2),
-            )
+            for h in range(2):
+                bank = turn_bank([P, 4, P])
+                for t in range(4):
+                    first = 512 * h + P * t
+                    nc.tensor.transpose(bank[:, t, :], picked[:, first : first + P], identity[:])
+                first = S * (unit % 2) + 512 * h
+                nc.scalar.copy(
+                    grouped_wd[unit // 2][:, first : first + 512].rearrange("p (n t) -> p n t", t=4),
+                    bank[:].rearrange("p t n -> p n t"),
+                )
 
         def quantise_wd(unit, count, kib):
             first = S * (unit % 2)
             codes = placed("wd_codes%d" % unit, [P, count * 2 * P], U32, kib)
             scales = held.tile([P, count * 2 * P], U8, name="wd_scales%d" % unit, align_bytes=64)
-            nc.vector.quantize_mx(
-                out=codes[:].bitcast(FP8X4), scales=scales[:], in_=grouped_wd[unit // 2][:, first : first + count * S]
-            )
+            calls = 2 if unit == 11 else 1
+            width = count * 2 * P // calls
+            for i in range(calls):
+                cols = slice(width * i, width * (i + 1))
+                nc.vector.quantize_mx(
+                    out=codes[:, cols].bitcast(FP8X4),
+                    scales=scales[:, cols],
+                    in_=grouped_wd[unit // 2][:, first + 4 * width * i : first + 4 * width * (i + 1)],
+                )
             for i in range(count):
                 stationary[unit + i] = (codes, scales, 2 * P * i)
 
@@ -317,7 +325,7 @@ def tile_list_robust_ct_sweep_kernel(
         update(2, range(2))
         quantise_wd(11, 1, 64)
         update(2, range(2, 3))
-        quantise_y(1, window_kib(11) + 2)
+        quantise_y(1, 2)
         for q in range(4):
             nc.sync.dma_start(
                 out_2[0:2, 4 * q : 4 * q + 4, :].bitcast(I32), y_planes_early[32 * q : 32 * q + 8, :].bitcast(I32)

from contextlib import ExitStack

import concourse.mybir as mybir
from concourse.masks import make_identity

K, T, S, M = 1536, 2048, 1024, 512
FLOPS = 2 * K * S * M * 2

F32 = mybir.dt.float32
BF16 = mybir.dt.bfloat16
I32 = mybir.dt.int32
U32 = mybir.dt.uint32
U16 = mybir.dt.uint16
U8 = mybir.dt.uint8
FP8X4 = mybir.dt.float8_e4m3fn_x4
ALU = mybir.AluOpType
ACT = mybir.ActivationFunctionType

P = 128
KIB = 1024
GP_PARTS = 1


def tile_list_robust_ct_sweep_kernel(
    tc, tab_words, tab_scales, offs, xb_words, xb_scales, x, b, lo, hi, g, wdT, out_0, out_1, out_2
):
    nc = tc.nc
    with ExitStack() as ctx:
        lists = ctx.enter_context(tc.tile_pool(name="lists", bufs=1))
        held = ctx.enter_context(tc.tile_pool(name="held", bufs=1))
        arena = ctx.enter_context(tc.tile_pool(name="arena", bufs=1))
        ring = ctx.enter_context(tc.tile_pool(name="ring", bufs=3))
        psum = ctx.enter_context(tc.psum_pool(name="psum", bufs=1))
        sum_banks = []
        turn_banks = []

        def sum_bank(shape):
            n = len(sum_banks)
            sum_banks.append(n)
            return psum.tile(shape, F32, name="sum_bank%d" % n, offset=2 * KIB * (n % 4))

        def turn_bank(shape):
            n = len(turn_banks)
            turn_banks.append(n)
            return psum.tile(shape, F32, name="turn_bank%d" % n, offset=2 * KIB * (4 + n % 4))

        def placed(name, shape, dtype, kib):
            return arena.tile(shape, dtype, name=name, offset=kib * KIB, align_bytes=64)

        offsets = lists.tile([P, S // 16], U16, name="offsets")
        nc.sync.dma_start(offsets[:], offs)

        tab_scale_window = placed("tab_scale_window", [P, T], U8, 176)
        nc.vector.memset(tab_scale_window[:].bitcast(I32), 0)
        xb_planes = held.tile([P, 3, M], U8, name="xb_planes", align_bytes=64)
        ray_rows = held.tile([P, M], F32, name="ray_rows")
        nc.vector.memset(ray_rows[:], 0.0)
        nc.vector.memset(xb_planes[:].bitcast(I32), 0)
        identity = held.tile([P, P], F32, name="identity")
        make_identity(nc, identity[:])

        def load_tab_words(a):
            window = placed("tab_window%d" % a, [P, T], I32, 8 * a)
            nc.sync.dma_start(window[:], tab_words[a].rearrange("p t i -> p (t i)").bitcast(I32))
            return window

        def load_tab_scales(q):
            nc.gpsimd.dma_start(
                tab_scale_window[32 * q : 32 * q + 12, :].bitcast(I32),
                tab_scales[:, 4 * q : 4 * q + 4, :].bitcast(I32),
            )

        def load_xb_scales(q):
            nc.sync.dma_start(
                xb_planes[32 * q : 32 * q + 4, :, :].bitcast(I32),
                xb_scales[:, 4 * q : 4 * q + 4, :].rearrange("a r e -> r a e").bitcast(I32),
            )

        def load_ray_rows(i, vec):
            nc.sync.dma_start(ray_rows[2 * i : 2 * i + 2, :], vec.rearrange("(h c) -> h c", h=2))

        def load_rows(name, src, group, kib):
            tile = placed(name, [P, 4, M], F32, kib)
            nc.sync.dma_start(tile[:], src[512 * group : 512 * (group + 1), :].rearrange("(p t) m -> p t m", t=4))
            return tile

        def wd_rows(group):
            return wdT[512 * group : 512 * (group + 1), :].rearrange("(p t) c -> p t c", t=4)

        def load_single(group, t, kib):
            tile = placed("wd_window%d_%d" % (group, t), [P, T], F32, kib)
            nc.sync.dma_start(tile[:], wd_rows(group)[:, t, :])
            return tile

        def load_pair(group, t, kib):
            tile = placed("wd_pair%d_%d" % (group, t), [P, 2, T], F32, kib)
            nc.sync.dma_start(tile[:], wd_rows(group)[:, t : t + 2, :])
            return tile

        WINDOW_KIB = 72

        def window_kib(unit):
            return WINDOW_KIB + 8 * unit

        windows = {}

        def load_windows(first, count):
            for unit in range(first, first + count):
                windows[unit] = load_single(unit // 4, unit % 4, window_kib(unit))

        for q in range(4):
            load_tab_scales(q)
        tab_windows = [load_tab_words(a) for a in range(2)]
        load_ray_rows(0, lo)
        load_ray_rows(1, hi)
        load_ray_rows(2, g)
        tab_windows.append(load_tab_words(2))
        load_xb_scales(0)
        load_xb_scales(1)
        xb_codes = held.tile([P, 3, M], I32, name="xb_codes", align_bytes=64)
        nc.sync.dma_start(xb_codes[:], xb_words.rearrange("a p e i -> p a (e i)").bitcast(I32))
        load_xb_scales(2)
        load_xb_scales(3)
        load_windows(0, 1)
        b_sb = [load_rows("b0", b, 0, 24)]
        load_windows(1, 1)
        b_sb.append(load_rows("b1", b, 1, 32))
        load_windows(2, 3)
        x_sb = [load_rows("x0", x, 0, 40)]
        load_windows(5, 3)
        x_sb.append(load_rows("x1", x, 1, 48))
        load_windows(8, 3)
        x_last = placed("x2", [P, 4, M], F32, 56)
        x_last_rows = x[1024:1536, :].rearrange("(p t) m -> p t m", t=4)
        nc.sync.dma_start(x_last[:, 0:2, :], x_last_rows[:, 0:2, :])
        load_windows(11, 1)
        nc.sync.dma_start(x_last[:, 2:4, :], x_last_rows[:, 2:4, :])
        x_sb.append(x_last)

        def dealt_view(tile):
            return tile[:].rearrange("p (h t q) -> p h q t", h=2, t=4)

        picked_words = [placed("picked_words%d" % a, [P, S], U32, 168 + 4 * a) for a in range(3)]
        picked_scales = held.tile([P, S], U8, name="picked_scales", align_bytes=64)
        for a in range(2):
            nc.vector.tensor_copy(dealt_view(picked_words[a]), tab_windows[a][:].bitcast(U32).indirect(offsets[:]))
        nc.vector.tensor_copy(dealt_view(picked_scales), tab_scale_window[:].indirect(offsets[:]))
        for h in range(2):
            nc.vector.tensor_copy(
                dealt_view(picked_words[2])[:, h], tab_windows[2][:].bitcast(U32).indirect(offsets[:, 32 * h : 32 * (h + 1)])
            )

        ray_bank = turn_bank([P, 4, P])
        for t in range(4):
            nc.tensor.transpose(ray_bank[:, t, :], ray_rows[:, t : M : 4], identity[:])
        ray_values = held.tile([P, 4, 6], F32, name="ray_values")
        nc.scalar.copy(ray_values[:], ray_bank[:, :, 0:6])

        grouped_wd = {}
        stationary = {}

        def gather_and_turn(unit):
            picked = ring.tile([P, S], F32, name="picked_wd")
            nc.vector.tensor_copy(dealt_view(picked), windows[unit][:].indirect(offsets[:]))
            if unit == 10:
                grouped_wd[unit // 2] = placed("grouped_wd_last", [P, 2 * S], BF16, 0)
            elif unit % 2 == 0:
                grouped_wd[unit // 2] = ring.tile([P, 2 * S], BF16, name="grouped_wd", align_bytes=64)
            for h in range(2):
                bank = turn_bank([P, 4, P])
                for t in range(4):
                    first = 512 * h + P * t
                    nc.tensor.transpose(bank[:, t, :], picked[:, first : first + P], identity[:])
                first = S * (unit % 2) + 512 * h
                nc.scalar.copy(
                    grouped_wd[unit // 2][:, first : first + 512].rearrange("p (n t) -> p n t", t=4),
                    bank[:].rearrange("p t n -> p n t"),
                )

        def quantise_wd(unit, count, kib):
            first = S * (unit % 2)
            codes = placed("wd_codes%d" % unit, [P, count * 2 * P], U32, kib)
            scales = held.tile([P, count * 2 * P], U8, name="wd_scales%d" % unit, align_bytes=64)
            calls = 2 if unit == 11 else 1
            width = count * 2 * P // calls
            for i in range(calls):
                cols = slice(width * i, width * (i + 1))
                nc.vector.quantize_mx(
                    out=codes[:, cols].bitcast(FP8X4),
                    scales=scales[:, cols],
                    in_=grouped_wd[unit // 2][:, first + 4 * width * i : first + 4 * width * (i + 1)],
                )
            for i in range(count):
                stationary[unit + i] = (codes, scales, 2 * P * i)

        def interleave(dst, src):
            nc.scalar.copy(
                dst[:].rearrange("p (c i t) -> p c t i", i=4, t=4),
                src[:].rearrange("p t (c i) -> p c t i", i=4),
            )

        grouped_h = []
        rounded_h = [held.tile([P, 4, M], BF16, name="h_rounded%d" % h) for h in range(2)]
        residual = []

        def residuals(h, ts):
            rows = b_sb[h]
            rounded = rounded_h[h]
            for t in ts:
                cols = slice(512 * h + P * t, 512 * h + P * (t + 1))
                acc = sum_bank([P, M])
                for a in range(3):
                    nc.tensor.matmul_mx(
                        out=acc[:],
                        lhsT=picked_words[a][:, cols].bitcast(FP8X4),
                        lhsT_scale=picked_scales[4 * a : P, cols],
                        rhs=xb_codes[:, a, :].bitcast(FP8X4),
                        rhs_scale=xb_planes[:, a, :],
                        start=(a == 0),
                        stop=(a == 2),
                    )
                nc.vector.tensor_tensor(rows[:, t, :], acc[:], rows[:, t, :], ALU.subtract)
                nc.gpsimd.tensor_scalar(
                    rows[:, t, :], rows[:, t, :], ray_values[:, t, 2 + h : 3 + h], ray_values[:, t, h : h + 1], ALU.min, ALU.max
                )
                nc.gpsimd.tensor_scalar(
                    rounded[:, t, :], rows[:, t, :], ray_values[:, t, 4 + h : 5 + h], 0.0, ALU.mult, ALU.add
                )

        def group_h(h, unit):
            grouped = placed("h_grouped%d" % h, [P, 4 * M], BF16, window_kib(unit) + 4)
            interleave(grouped, rounded_h[h])
            grouped_h.append(grouped)

        def quantise_h(h, unit):
            codes = placed("h_codes%d" % h, [P, M], U32, window_kib(unit) + 2)
            scales = held.tile([P, M], U8, name="h_scales%d" % h, align_bytes=64)
            nc.vector.quantize_mx(out=codes[:].bitcast(FP8X4), scales=scales[:], in_=grouped_h[h][:])
            residual.append((codes, scales))

        y_planes_early = held.tile([P, M], U8, name="y_planes_early", align_bytes=64)
        y_plane_last = held.tile([P, M], U8, name="y_plane_last", align_bytes=64)
        grouped_y = []

        y_sb = {0: x_sb[0], 1: x_sb[1]}

        def update(group, ts):
            rows = y_sb[group]
            out_rows = out_0[512 * group : 512 * (group + 1), :].rearrange("(p t) m -> p t m", t=4)
            for t in ts:
                codes, scales, first = stationary[4 * group + t]
                acc = sum_bank([P, M])
                for h in range(2):
                    cols = slice(first + P * h, first + P * (h + 1))
                    nc.tensor.matmul_mx(
                        out=acc[:],
                        lhsT=codes[:, cols].bitcast(FP8X4),
                        lhsT_scale=scales[:, cols],
                        rhs=residual[h][0][:].bitcast(FP8X4),
                        rhs_scale=residual[h][1][:],
                        start=(h == 0),
                        stop=(h == 1),
                    )
                if group < 2:
                    staged = placed("staged_y%d_%d" % (group, t), [P, M], F32, 8 + 8 * group + 2 * t)
                    nc.scalar.copy(staged[:], acc[:])
                    for half in range(GP_PARTS):
                        cols = slice(half * M // GP_PARTS, (half + 1) * M // GP_PARTS)
                        nc.gpsimd.tensor_tensor(rows[:, t, cols], rows[:, t, cols], staged[:, cols], ALU.subtract)
                    if t == 3:
                        nc.sync.dma_start(out_rows, rows[:])
                else:
                    nc.vector.tensor_tensor(rows[:, t, :], x_sb[group][:, t, :], acc[:], ALU.subtract)
                    if t % 2 == 1:
                        nc.sync.dma_start(out_rows[:, t - 1 : t + 1, :], rows[:, t - 1 : t + 1, :])

        def group_y(group, kib):
            rows = y_sb[group]
            grouped = placed("y_grouped%d" % group, [P, 4 * M], BF16, kib)
            if group < 2:
                interleave(grouped, rows)
            else:
                dst = grouped[:].rearrange("p (c i t) -> p c t i", i=4, t=4)
                src = rows[:].rearrange("p t (c i) -> p c t i", i=4)
                nc.scalar.copy(dst[:, 0:48], src[:, 0:48])
                nc.vector.tensor_copy(dst[:, 48:128], src[:, 48:128])
            grouped_y.append(grouped)

        def quantise_y(group, kib):
            codes = placed("y_codes%d" % group, [P, M], I32, kib)
            plane = y_plane_last[:] if group == 2 else y_planes_early[4 * group : P, :]
            nc.vector.quantize_mx(out=codes[:].bitcast(FP8X4), scales=plane, in_=grouped_y[group][:])
            nc.sync.dma_start(out_1[group].rearrange("p m t -> p (m t)").bitcast(I32), codes[:])

        gather_and_turn(0)
        residuals(0, range(4))
        gather_and_turn(1)
        group_h(0, 1)
        residuals(1, range(4))
        gather_and_turn(2)
        gather_and_turn(3)
        quantise_wd(0, 2, window_kib(3))
        quantise_h(0, 3)
        gather_and_turn(4)
        group_h(1, 4)
        gather_and_turn(5)
        quantise_wd(2, 2, window_kib(5))
        quantise_h(1, 5)
        update(0, range(4))
        gather_and_turn(6)
        quantise_wd(4, 2, window_kib(6))
        gather_and_turn(7)
        gather_and_turn(8)
        quantise_wd(6, 2, window_kib(8))
        group_y(0, window_kib(8) + 4)
        update(1, range(4))
        gather_and_turn(9)
        gather_and_turn(10)
        quantise_wd(8, 2, window_kib(10))
        quantise_y(0, window_kib(10) + 2)
        group_y(1, window_kib(10) + 4)
        gather_and_turn(11)
        quantise_wd(10, 1, window_kib(11))
        y_sb[2] = placed("y2", [P, 4, M], F32, window_kib(11) + 4)
        update(2, range(2))
        quantise_wd(11, 1, 64)
        update(2, range(2, 3))
        quantise_y(1, 2)
        for q in range(4):
            nc.sync.dma_start(
                out_2[0:2, 4 * q : 4 * q + 4, :].bitcast(I32), y_planes_early[32 * q : 32 * q + 8, :].bitcast(I32)
            )
        update(2, range(3, 4))
        group_y(2, 68)
        quantise_y(2, 66)
        for q in range(4):
            nc.sync.dma_start(
                out_2[2, 4 * q : 4 * q + 4, :].bitcast(I32), y_plane_last[32 * q : 32 * q + 4, :].bitcast(I32)
            )
